import numpy as np, ml_dtypes
CORES = [48,51,52,55]
N = 4
BF = ml_dtypes.bfloat16
def gentries(a):
    return np.ascontiguousarray(a.reshape(8, 16, -1).transpose(0, 2, 1)).reshape(8, -1)
def gtable(e):
    e = np.asarray(e); return np.ascontiguousarray(e.reshape(8, -1, 16).transpose(0, 2, 1)).reshape(128, -1).astype(np.int32)
D, UG, B, A, NB, KG = 2, 16, 6, 2, 64, 32
U, V, E, S, K = 8 * UG, 2 ** B, 2 ** (A * B), 16 * NB, 8 * KG // N
def stored(c):
    return np.ascontiguousarray(c.reshape(N, 8, UG, NB, 16).transpose(0, 1, 4, 3, 2)).reshape(N, 128, -1).astype(np.int32)
def unstored(x):
    return np.ascontiguousarray(x.reshape(N, 8, 16, NB, UG).transpose(0, 1, 4, 3, 2)).reshape(N, U, S).astype(np.int64)
def pack(t, c, gv, wr):
    return {"tb": t.reshape(N, 8, -1).astype(np.float32).astype(BF), "x": stored(c), "give": np.stack([gtable(v.reshape(8, -1)) for v in gv]), "wires": np.stack([gtable(v.reshape(8, -1)) for v in wr])}
def draw(rng):
    return rng.integers(0, V, (N, 8, D, UG, E)), rng.integers(0, V, (N, U, S)), rng.integers(0, U, (N, 8, D, KG)), rng.integers(0, N * K, (N, 8, D, A, UG))
def setup_inputs(rng):
    return pack(*draw(rng))
def setup_inputs_ends(rng):
    t, c, gv, wr = draw(rng)
    t = rng.integers(0, 2, t.shape) * (V - 1); t[..., 0] = 0; t[..., E - 1] = V - 1; c = rng.integers(0, 2, c.shape) * (V - 1); c[:, :, 0] = 0; c[:, :, S - 1] = V - 1
    gv = rng.choice(np.array([0, UG - 1, UG, 7 * UG, U - 1]), gv.shape); wr = rng.choice(np.array([0, K - 1, K, N * K - K, N * K - 1]), wr.shape)
    return pack(t, c, gv, wr)
def setup_inputs_one(rng):
    t, c, gv, wr = draw(rng)
    gv[:] = gv[..., :1].copy(); wr[:] = wr[:, :, :, :1].copy(); q = rng.integers(0, N); wr[q] = wr[q][..., :1].copy()
    return pack(t, c, gv, wr)
def setup_inputs_next(rng):
    t, c, gv, wr = draw(rng)
    i = rng.integers(0, 2, (N, 8, D, UG, 1)) * (A - 1); t = (np.arange(E) >> (B * (A - 1 - i))) & (V - 1)
    wr = wr % K + K * ((np.arange(N) + 1) % N).reshape(N, 1, 1, 1, 1)
    return pack(t, c, gv, wr)
def setup_inputs_spread(rng):
    t, c, gv, wr = draw(rng)
    t = t >> rng.integers(0, B + 1, (N, 8, D, UG, 1)); c = c >> rng.integers(0, B + 1, (N, U, 1))
    gv = (rng.random(gv.shape) ** 3 * U).astype(np.int64); wr = (rng.random(wr.shape) ** 3 * (N * K)).astype(np.int64)
    return pack(t, c, gv, wr)
def check_inputs(d):
    bad = []
    for name, top in (("x", V), ("give", U), ("wires", N * K)):
        if not ((d[name] >= 0) & (d[name] < top)).all(): bad.append(name)
    t = d["tb"].astype(np.float32)
    if not ((t >= 0) & (t < V) & (np.floor(t) == t)).all(): bad.append("tb")
    return bad
def reference(tb, x, give, wires):
    t = tb.astype(np.float32).astype(np.int64).reshape(N, 8, D, UG, E)
    gv = np.stack([gentries(v) for v in give]).reshape(N, 8 * D * KG).reshape(N, 8, D, KG)
    wr = np.stack([gentries(v) for v in wires]).reshape(N, 8, D, A, UG)
    c = unstored(x)
    for l in range(D):
        lines = np.zeros((N, N * K, S), np.int64); new = np.zeros((N, U, S), np.int64)
        for q in range(N):
            lines[:, q * K:(q + 1) * K] = c[q][gv[q, :, l].reshape(-1)].reshape(N, K, S)
        for r in range(N):
            a = np.zeros((8, UG, S), np.int64)
            for i in range(A):
                a = a * V + lines[r][wr[r, :, l, i]]
            new[r] = np.take_along_axis(t[r, :, l], a, axis=2).reshape(U, S)
        c = new
    return {"y": np.asarray(stored(c), np.float32)}

@@ -1,0 +1,345 @@
+from concourse.bass import DstId, RemoteDMATransfer
+from concourse.mybir import AluOpType as OP, ActivationFunctionType as ACT
+
+NCH = 4
+CS = 256
+TS = 128
+
+SCRATCH = {
+    "xi": ("sbuf", [128, 1024], "int32"),
+    "xb": ("sbuf", [128, 1024], "bfloat16"),
+    "yt": ("sbuf", [128, 1024], "bfloat16"),
+    "gs": ("sbuf", [128, 4], "int32"),
+    "gl": ("sbuf", [128, 16], "int32"),
+    "giv": ("sbuf", [128, 4], "float32"),
+    "wi": ("sbuf", [128, 4], "int32"),
+    "wf": ("sbuf", [128, 4], "float32"),
+    "pcol": ("sbuf", [128, 1], "int32"),
+    "pmi": ("sbuf", [128, 1], "int32"),
+    "kbi": ("sbuf", [128, 1], "int32"),
+    "pmf": ("sbuf", [128, 1], "float32"),
+    "kbf": ("sbuf", [128, 2], "float32"),
+    "col16": ("sbuf", [128, 16], "float32"),
+    "k16": ("sbuf", [128, 16], "float32"),
+    "diff": ("sbuf", [128, 128], "float32"),
+    "rdiff": ("sbuf", [128, 128], "float32"),
+    "iotn": ("sbuf", [128, 128], "bfloat16"),
+    "iotl": ("sbuf", [128, 256], "bfloat16"),
+    "ident": ("sbuf", [128, 128], "bfloat16"),
+    "pm": ("sbuf", [128, 512], "bfloat16"),
+    "lm": ("sbuf", [128, 2048], "bfloat16"),
+    "rm": ("sbuf", [128, 128], "bfloat16"),
+    "vt": ("sbuf", [128, 1024], "bfloat16"),
+    "vb": ("sbuf", [128, 512], "bfloat16"),
+    "gt": ("sbuf", [128, 512], "bfloat16"),
+    "w": ("sbuf", [128, 1024], "bfloat16"),
+    "c0": ("sbuf", [128, 4096], "bfloat16"),
+    "c1": ("sbuf", [128, 4096], "bfloat16"),
+    "tab0": ("sbuf", [128, 4096], "bfloat16"),
+    "tab1": ("sbuf", [128, 4096], "bfloat16"),
+    "off0": ("sbuf", [128, 1024], "uint16"),
+    "off1": ("sbuf", [128, 1024], "uint16"),
+    "ga0": ("sbuf", [128, 16384], "bfloat16"),
+    "ga1": ("sbuf", [128, 16384], "bfloat16"),
+    "ys": ("sbuf", [128, 1024], "float32"),
+    "psv": ("psum", [128, 512], "float32"),
+    "psw": ("psum", [128, 512], "float32"),
+    "psf0": ("psum", [128, 512], "float32"),
+    "psf1": ("psum", [128, 512], "float32"),
+    "psa0": ("psum", [128, 512], "float32"),
+    "psa1": ("psum", [128, 512], "float32"),
+    "psc0": ("psum", [128, 512], "float32"),
+    "psc1": ("psum", [128, 512], "float32"),
+}
+SEMAPHORES = (["dx0", "dxr", "dgv", "dwr", "dt0", "dt1", "dy", "io1", "io2", "vi", "vf", "vk", "vid", "vpm", "vlm", "vrm",
+               "vwf", "vvt0", "vvt1", "vgiv", "vgt0", "vgt1", "pv0", "pv1", "sv0", "sv1", "pwv", "pws", "pw1", "swv", "sws",
+               "sw1", "agv", "loc"]
+              + ["%s%d" % (a, c) for c in range(NCH) for a in ("cv", "tr", "pf", "ce", "ac", "bc", "sc", "sy")]
+              + ["%s%d%d" % (a, l, c) for l in range(2) for c in range(NCH) for a in ("pa", "ea", "gv", "gsc", "pd")])
+
+
+def rank_program(g, core, T, topo):
+    rank = T.rank_of(core)
+    if rank is None:
+        return
+    V, S, P, Y = g.vector, g.scalar, g.tensor, g.sync
+    sem = T.sem
+    others = [c for c in T.cores if c != core]
+    n_oth = len(others)
+    engs = topo.engines(core, others[0])
+    for c in others:
+        engs = [e for e in engs if e in topo.engines(core, c)]
+    engs = engs[::2]
+    ne = len(engs)
+    emask = sum(1 << e for e in engs)
+    ids = []
+    for c in others:
+        a = topo.addr(c)
+        ids.append(DstId(rid=a[0], pnc=a[1]))
+
+    def bcast(src, dst, name):
+        g.remote_dma_fused([RemoteDMATransfer(dst_ids=ids, dma_engine_mask=emask, remote_sem=sem[name],
+                                              srcs=[src], dsts=[dst] * n_oth)], local_sem=sem.loc)
+
+    own = rank * 1024
+    psf, psa, psc = [T.psf0, T.psf1], [T.psa0, T.psa1], [T.psc0, T.psc1]
+    cb, tab, off, ga = [T.c0, T.c1], [T.tab0, T.tab1], [T.off0, T.off1], [T.ga0, T.ga1]
+    psw = [[T.psc0, T.psc1, T.psw, T.psa1], [T.psw] * 4]
+
+    Y.dma_start(T.xi[:, 0:CS], T.x[:, 0:CS]).then_inc(sem.dx0, 16)
+    S.dma_start(T.gs[:], T.give[:]).then_inc(sem.dgv, 16)
+    S.dma_start(T.wi[:], T.wires[:]).then_inc(sem.dwr, 16)
+    Y.dma_start(T.xi[:, CS:1024], T.x[:, CS:1024]).then_inc(sem.dxr, 16)
+    Y.dma_start(T.tab0[:], T.tb[:, 0:65536]).then_inc(sem.dt0, 16)
+
+    g.iota(T.pcol[:], [[1, 1]], 0, 1).then_inc(sem.io1, 1)
+    g.iota(T.diff[:], [[1, 128]], 0, -1, allow_small_or_imprecise_dtypes=True).then_inc(sem.io1, 1)
+    g.iota(T.col16[:], [[1, 16]], 0, 0, allow_small_or_imprecise_dtypes=True).then_inc(sem.io1, 1)
+    g.iota(T.iotl[:], [[16, 2], [32, 8], [1, 16]], 0, 0, allow_small_or_imprecise_dtypes=True).then_inc(sem.io2, 1)
+    g.iota(T.iotn[:], [[1, 128]], 0, 0, allow_small_or_imprecise_dtypes=True).then_inc(sem.io2, 1)
+    g.iota(T.rdiff[:], [[1, 16], [16, 8]], 0, -1, allow_small_or_imprecise_dtypes=True).then_inc(sem.io2, 1)
+    g.wait_ge(sem.dgv, 16)
+    bcast(T.gs[:], T.gl[:, 4 * rank:4 * rank + 4], "agv")
+    for l in range(2):
+        for c in range(NCH):
+            g.wait_ge(sem["%s%d" % ("sc" if l else "ce", c)], 1)
+            a = own + c * CS
+            bcast(cb[l][:, a:a + CS], cb[l][:, a:a + CS], "%s%d" % ("bc" if l else "ac", c))
+    g.wait_ge(sem.loc, ne * (1 + 2 * NCH))
+
+    def convert(c):
+        V.tensor_copy(T.xb[:, c * CS:(c + 1) * CS], T.xi[:, c * CS:(c + 1) * CS]).then_inc(sem["cv%d" % c], 1)
+
+    def turn(c):
+        V.wait_ge(sem["cv%d" % c], 1)
+        for bp in range(8):
+            i0 = c * CS + 32 * bp
+            V.transpose(T.yt[:, c * CS + bp:(c + 1) * CS:8], T.xb[:, i0:i0 + 32]).then_inc(sem["tr%d" % c], 1)
+
+    def masks(lo, hi):
+        for u in range(lo, hi):
+            V.tensor_scalar(T.lm[:, 128 * u:128 * u + 128], T.ident[:], T.k16[:, u:u + 1], None, OP.mult).then_inc(sem.vlm, 1)
+
+    def onehot_give(l):
+        for k in (2 * l, 2 * l + 1):
+            V.tensor_scalar(T.gt[:, 128 * k:128 * k + 128], T.iotn[:], T.giv[:, k:k + 1], None, OP.is_equal).then_inc(sem["vgt%d" % l], 1)
+
+    def fix(c):
+        P.wait_ge(sem["tr%d" % c], 8)
+        if c == 0:
+            P.wait_ge(sem.vpm, 4)
+        if c >= 2:
+            P.wait_ge(sem["ce%d" % (c - 2)], 1)
+        for h in range(2):
+            for g2 in range(2):
+                k = 2 * g2 + h
+                m = P.matmul(psf[c % 2][:, 128 * h:128 * h + 128], T.pm[:, 128 * k:128 * k + 128],
+                             T.yt[:, c * CS + 128 * g2:c * CS + 128 * g2 + 128], g2 == 0, g2 == 1)
+                if g2 == 1:
+                    m.then_inc(sem["pf%d" % c], 1)
+
+    def compose_v(l):
+        P.wait_ge(sem["vvt%d" % l], 2)
+        for kh in range(2):
+            for i in range(2):
+                a = (2 * l + i) * 256 + 128 * kh
+                m = P.matmul(T.psv[:, l * 256 + 128 * kh:l * 256 + 128 * kh + 128], T.vt[:, a:a + 128], T.ident[:], i == 0, i == 1)
+                if i == 1:
+                    m.then_inc(sem["pv%d" % l], 1)
+
+    def compose_w(l):
+        P.wait_ge(sem["vgt%d" % l], 2)
+        P.wait_ge(sem["sv%d" % l], 1)
+        for q in range(4):
+            if l and q:
+                P.wait_ge(sem.pw1, q)
+            a = 128 * q if l else 0
+            for kh in range(2):
+                m = P.matmul(psw[l][q][:, a:a + 128],
+                             T.gt[32 * q:32 * q + 32, (2 * l + kh) * 128:(2 * l + kh) * 128 + 128],
+                             T.vb[32 * q:32 * q + 32, l * 256 + 128 * kh:l * 256 + 128 * kh + 128], kh == 0, kh == 1)
+            m.then_inc(sem["pw1" if l else ("pwv" if q < 2 else "pws")], 1)
+
+    def addresses(l, c):
+        if c == 0:
+            if l == 0:
+                P.wait_ge(sem.swv, 2)
+                P.wait_ge(sem.sws, 2)
+            else:
+                P.wait_ge(sem.sw1, 1)
+        P.wait_ge(sem["%s%d" % ("ce" if l == 0 else "sc", c)], 1)
+        P.wait_ge(sem["%s%d" % ("ac" if l == 0 else "bc", c)], ne * n_oth)
+        k = l * NCH + c - 2
+        if k >= 0:
+            P.wait_ge(sem["ea%d%d" % (k // NCH, k % NCH)], 1)
+        for q in range(4):
+            m = P.matmul(psa[c % 2][:, 0:CS], T.w[:, (4 * l + q) * 128:(4 * l + q) * 128 + 128],
+                         cb[l][:, q * 1024 + c * CS:q * 1024 + (c + 1) * CS], q == 0, q == 3)
+        m.then_inc(sem["pa%d%d" % (l, c)], 1)
+
+    def pick(l, c):
+        if c == 0:
+            P.wait_ge(sem.vrm if l else sem.vlm, 1 if l else 16)
+        k = l * NCH + c - 2
+        if k >= 0:
+            P.wait_ge(sem["%s%d" % ("sc" if k < NCH else "sy", k % NCH)], 1)
+        for h in range(2):
+            P.wait_ge(sem["%s%d%d" % ("gv" if h == 0 else "gsc", l, c)], 1)
+            j0 = (2 * c + h) * 2048
+            for u in range(16):
+                src = ga[l][:, j0 + u:j0 + 2048:16]
+                if l == 0:
+                    m = P.matmul(psc[c % 2][:, 128 * h:128 * h + 128], T.lm[:, 128 * u:128 * u + 128], src, u == 0, u == 15)
+                else:
+                    m = P.matmul(psc[c % 2][:, 16 * h + u:256:32], src, T.rm[:, 8 * u:8 * u + 8], True, True)
+            m.then_inc(sem["pd%d%d" % (l, c)], 1)
+
+    def evac_addr(l, c):
+        V.wait_ge(sem["pa%d%d" % (l, c)], 1)
+        V.tensor_copy(off[l][:, c * CS:(c + 1) * CS], psa[c % 2][:, 0:CS]).then_inc(sem["ea%d%d" % (l, c)], 1)
+
+    def gather(l, c, h):
+        q = S if h else V
+        q.wait_ge(sem["ea%d%d" % (l, c)], 1)
+        if c == 0:
+            q.wait_ge(sem["dt%d" % l], 16)
+        j0 = (2 * c + h) * 2048
+        o0 = c * CS + h * TS
+        win = tab[l][:, 0:4096].indirect(off[l][:, o0:o0 + TS])
+        if h == 0:
+            V.tensor_copy(ga[l][:, j0:j0 + 2048], win).then_inc(sem["gv%d%d" % (l, c)], 1)
+        else:
+            S.activation(ga[l][:, j0:j0 + 2048], win, ACT.Copy).then_inc(sem["gsc%d%d" % (l, c)], 1)
+
+    def s_c0(c):
+        S.wait_ge(sem["pf%d" % c], 2)
+        S.activation(T.c0[:, own + c * CS:own + (c + 1) * CS], psf[c % 2][:, 0:CS], ACT.Copy).then_inc(sem["ce%d" % c], 1)
+
+    def s_out(l, c):
+        S.wait_ge(sem["pd%d%d" % (l, c)], 2)
+        dst = T.ys[:, c * CS:(c + 1) * CS] if l else T.c1[:, own + c * CS:own + (c + 1) * CS]
+        S.activation(dst, psc[c % 2][:, 0:CS], ACT.Copy).then_inc(sem["%s%d" % ("sy" if l else "sc", c)], 1)
+
+    V.wait_ge(sem.io1, 3)
+    V.tensor_scalar(T.pmi[:], T.pcol[:], 15, None, OP.bitwise_and).then_inc(sem.vi, 1)
+    V.tensor_scalar(T.kbi[:], T.pcol[:], 4, 1, OP.logical_shift_right, OP.bitwise_and).then_inc(sem.vi, 1)
+    V.tensor_scalar(T.ident[:], T.diff[:], 0.0, None, OP.is_equal).then_inc(sem.vid, 1)
+    V.wait_ge(sem.vi, 2)
+    V.tensor_copy(T.pmf[:], T.pmi[:]).then_inc(sem.vf, 1)
+    V.tensor_copy(T.kbf[:, 1:2], T.kbi[:]).then_inc(sem.vf, 1)
+    V.tensor_scalar(T.kbf[:, 0:1], T.kbi[:], -1.0, 1.0, OP.mult, OP.add).then_inc(sem.vf, 1)
+    V.wait_ge(sem.vf, 3)
+    for g2 in range(2):
+        for h in range(2):
+            k = 2 * g2 + h
+            V.tensor_scalar(T.pm[:, 128 * k:128 * k + 128], T.diff[:], float(16 * (g2 - h)), T.kbf[:, h:h + 1],
+                            OP.is_equal, OP.mult).then_inc(sem.vpm, 1)
+    V.tensor_scalar(T.k16[:], T.col16[:], T.pmf[:], None, OP.is_equal).then_inc(sem.vk, 1)
+    V.wait_ge(sem.io2, 3)
+    V.tensor_scalar(T.rm[:], T.rdiff[:], 0.0, None, OP.is_equal).then_inc(sem.vrm, 1)
+    V.wait_ge(sem.dwr, 16)
+    V.tensor_copy(T.wf[:], T.wi[:]).then_inc(sem.vwf, 1)
+    V.wait_ge(sem.vwf, 1)
+    for l in range(2):
+        for i in range(2):
+            k = 2 * l + i
+            V.tensor_scalar(T.vt[:, 256 * k:256 * k + 256], T.iotl[:], T.wf[:, k:k + 1], 64.0 if i == 0 else 1.0,
+                            OP.is_equal, OP.mult).then_inc(sem["vvt%d" % l], 1)
+    V.wait_ge(sem.dx0, 16)
+    convert(0)
+    turn(0)
+    V.wait_ge(sem.vk, 1)
+    V.wait_ge(sem.vid, 1)
+    masks(0, 8)
+    V.wait_ge(sem.pf0, 2)
+    V.tensor_copy(T.c0[:, own:own + CS], T.psf0[:, 0:CS]).then_inc(sem.ce0, 1)
+    masks(8, 16)
+    V.wait_ge(sem.dxr, 16)
+    for c in range(1, NCH):
+        convert(c)
+    V.wait_ge(sem.dgv, 16)
+    V.wait_ge(sem.agv, ne * n_oth)
+    for q in range(4):
+        r0 = 32 * rank
+        src = T.gs[r0:r0 + 32, 0:4] if q == rank else T.gl[r0:r0 + 32, 4 * q:4 * q + 4]
+        V.tensor_copy(T.giv[32 * q:32 * q + 32, 0:4], src).then_inc(sem.vgiv, 1)
+    V.wait_ge(sem.vgiv, 4)
+    onehot_give(0)
+    turn(1)
+    V.wait_ge(sem.pwv, 2)
+    for q in range(2):
+        V.tensor_copy(T.w[:, 128 * q:128 * q + 128], psw[0][q][:, 0:128]).then_inc(sem.swv, 1)
+    turn(2)
+    onehot_give(1)
+    turn(3)
+    for l in range(2):
+        for c in range(NCH):
+            evac_addr(l, c)
+            gather(l, c, 0)
+
+    S.wait_ge(sem.pv0, 2)
+    S.wait_ge(sem.pv1, 2)
+    for l in range(2):
+        S.activation(T.vb[:, 256 * l:256 * l + 256], T.psv[:, 256 * l:256 * l + 256], ACT.Copy).then_inc(sem["sv%d" % l], 1)
+    S.wait_ge(sem.pws, 2)
+    for q in (2, 3):
+        S.activation(T.w[:, 128 * q:128 * q + 128], psw[0][q][:, 0:128], ACT.Copy).then_inc(sem.sws, 1)
+    s_c0(1)
+    s_c0(2)
+    gather(0, 0, 1)
+    s_c0(3)
+    gather(0, 1, 1)
+    S.wait_ge(sem.pw1, 4)
+    S.activation(T.w[:, 512:1024], T.psw[:], ACT.Copy).then_inc(sem.sw1, 1)
+    s_out(0, 0)
+    gather(0, 2, 1)
+    s_out(0, 1)
+    gather(0, 3, 1)
+    s_out(0, 2)
+    gather(1, 0, 1)
+    s_out(0, 3)
+    gather(1, 1, 1)
+    s_out(1, 0)
+    gather(1, 2, 1)
+    s_out(1, 1)
+    gather(1, 3, 1)
+    s_out(1, 2)
+    s_out(1, 3)
+
+    P.wait_ge(sem.vid, 1)
+    compose_v(0)
+    compose_v(1)
+    fix(0)
+    compose_w(0)
+    fix(1)
+    fix(2)
+    addresses(0, 0)
+    fix(3)
+    compose_w(1)
+    addresses(0, 1)
+    pick(0, 0)
+    addresses(0, 2)
+    pick(0, 1)
+    addresses(0, 3)
+    pick(0, 2)
+    addresses(1, 0)
+    pick(0, 3)
+    addresses(1, 1)
+    pick(1, 0)
+    addresses(1, 2)
+    pick(1, 1)
+    addresses(1, 3)
+    pick(1, 2)
+    pick(1, 3)
+
+    Y.wait_ge(sem.ea00, 1)
+    Y.dma_start(T.tab1[:], T.tb[:, 65536:131072]).then_inc(sem.dt1, 16)
+    for c in range(NCH):
+        last = c == NCH - 1
+        Y.wait_ge(sem["sy%d" % c], 1)
+        if last:
+            S.wait_ge(sem["sy%d" % c], 1)
+        for gg in range(8):
+            q = S if last and gg % 2 else Y
+            q.dma_start(T.y[16 * gg:16 * gg + 16, c * CS:(c + 1) * CS], T.ys[:, c * CS + 32 * gg:c * CS + 32 * gg + 32]).then_inc(sem.dy, 16)
+    Y.wait_ge(sem.dy, 16 * 8 * NCH)

@@ -4,6 +4,7 @@ from concourse.mybir import AluOpType as OP, ActivationFunctionType as ACT
 NCH = 4
 CS = 256
 TS = 128
+SM = 12
 
 SCRATCH = {
     "xi": ("sbuf", [128, 1024], "int32"),
@@ -42,6 +43,7 @@ SCRATCH = {
     "ga0": ("sbuf", [128, 16384], "bfloat16"),
     "ga1": ("sbuf", [128, 16384], "bfloat16"),
     "ys": ("sbuf", [128, 1024], "float32"),
+    "yl": ("sbuf", [128, 256], "float32"),
     "psv": ("psum", [128, 512], "float32"),
     "psw": ("psum", [128, 512], "float32"),
     "psf0": ("psum", [128, 512], "float32"),
@@ -51,11 +53,13 @@ SCRATCH = {
     "psc0": ("psum", [128, 512], "float32"),
     "psc1": ("psum", [128, 512], "float32"),
 }
-SEMAPHORES = (["dx0", "dxr", "dgv", "dwr", "dt0", "dt1", "dy", "io1", "io2", "vi", "vf", "vk", "vid", "vpm", "vlm", "vrm",
-               "vwf", "vvt0", "vvt1", "vgiv", "vgt0", "vgt1", "pv0", "pv1", "sv0", "sv1", "pwv", "pws", "pw1", "swv", "sws",
-               "sw1", "agv", "loc"]
-              + ["%s%d" % (a, c) for c in range(NCH) for a in ("cv", "tr", "pf", "ce", "ac", "bc", "sc", "sy")]
-              + ["%s%d%d" % (a, l, c) for l in range(2) for c in range(NCH) for a in ("pa", "ea", "gv", "gsc", "pd")])
+SEMAPHORES = (["dx0", "dxr", "dgv", "dwr", "dt0", "dt1", "dy", "iop", "iod", "iol", "ion", "ior", "vi", "vf", "vk", "vid",
+               "vpm", "vlm", "slm", "vrm", "vwf", "vvt0", "vvt1", "vgiv", "vgt0", "vgt1", "pv0", "pv1", "sv0", "sv1",
+               "pwv", "pws", "pw1", "swv", "sws", "sw1", "agv", "loc", "cv0", "cv1", "cv2", "tr0", "tr1", "tr2"]
+              + ["%s%d" % (a, c) for c in range(NCH) for a in ("pf", "ce", "ac", "bc", "sc")]
+              + ["%s%d%d" % (a, l, c) for l in range(2) for c in range(NCH) for a in ("pa", "ea")]
+              + ["%s%d%d" % (a, l, c) for l in range(2) for c in range(NCH + l) for a in ("gv", "gs", "pd")]
+              + ["sy%d" % c for c in range(NCH + 1)])
 
 
 def rank_program(g, core, T, topo):
@@ -69,7 +73,6 @@ def rank_program(g, core, T, topo):
     engs = topo.engines(core, others[0])
     for c in others:
         engs = [e for e in engs if e in topo.engines(core, c)]
-    engs = engs[::2]
     ne = len(engs)
     emask = sum(1 << e for e in engs)
     ids = []
@@ -85,6 +88,7 @@ def rank_program(g, core, T, topo):
     psf, psa, psc = [T.psf0, T.psf1], [T.psa0, T.psa1], [T.psc0, T.psc1]
     cb, tab, off, ga = [T.c0, T.c1], [T.tab0, T.tab1], [T.off0, T.off1], [T.ga0, T.ga1]
     psw = [[T.psc0, T.psc1, T.psw, T.psa1], [T.psw] * 4]
+    psv = [T.psv, T.psa0]
 
     Y.dma_start(T.xi[:, 0:CS], T.x[:, 0:CS]).then_inc(sem.dx0, 16)
     S.dma_start(T.gs[:], T.give[:]).then_inc(sem.dgv, 16)
@@ -92,58 +96,61 @@ def rank_program(g, core, T, topo):
     Y.dma_start(T.xi[:, CS:1024], T.x[:, CS:1024]).then_inc(sem.dxr, 16)
     Y.dma_start(T.tab0[:], T.tb[:, 0:65536]).then_inc(sem.dt0, 16)
 
-    g.iota(T.pcol[:], [[1, 1]], 0, 1).then_inc(sem.io1, 1)
-    g.iota(T.diff[:], [[1, 128]], 0, -1, allow_small_or_imprecise_dtypes=True).then_inc(sem.io1, 1)
-    g.iota(T.col16[:], [[1, 16]], 0, 0, allow_small_or_imprecise_dtypes=True).then_inc(sem.io1, 1)
-    g.iota(T.iotl[:], [[16, 2], [32, 8], [1, 16]], 0, 0, allow_small_or_imprecise_dtypes=True).then_inc(sem.io2, 1)
-    g.iota(T.iotn[:], [[1, 128]], 0, 0, allow_small_or_imprecise_dtypes=True).then_inc(sem.io2, 1)
-    g.iota(T.rdiff[:], [[1, 16], [16, 8]], 0, -1, allow_small_or_imprecise_dtypes=True).then_inc(sem.io2, 1)
+    lax = {"allow_small_or_imprecise_dtypes": True}
+    g.iota(T.pcol[:], [[1, 1]], 0, 1).then_inc(sem.iop, 1)
+    g.iota(T.col16[:], [[1, 16]], 0, 0, **lax).then_inc(sem.iop, 1)
+    g.iota(T.diff[:], [[1, 128]], 0, -1, **lax).then_inc(sem.iod, 1)
+    g.iota(T.iotl[:], [[16, 2], [32, 8], [1, 16]], 0, 0, **lax).then_inc(sem.iol, 1)
     g.wait_ge(sem.dgv, 16)
     bcast(T.gs[:], T.gl[:, 4 * rank:4 * rank + 4], "agv")
+    g.iota(T.iotn[:], [[1, 128]], 0, 0, **lax).then_inc(sem.ion, 1)
     for l in range(2):
         for c in range(NCH):
             g.wait_ge(sem["%s%d" % ("sc" if l else "ce", c)], 1)
             a = own + c * CS
             bcast(cb[l][:, a:a + CS], cb[l][:, a:a + CS], "%s%d" % ("bc" if l else "ac", c))
+            if l == 0 and c == 0:
+                g.iota(T.rdiff[:], [[1, 16], [16, 8]], 0, -1, **lax).then_inc(sem.ior, 1)
     g.wait_ge(sem.loc, ne * (1 + 2 * NCH))
 
-    def convert(c):
-        V.tensor_copy(T.xb[:, c * CS:(c + 1) * CS], T.xi[:, c * CS:(c + 1) * CS]).then_inc(sem["cv%d" % c], 1)
-
-    def turn(c):
-        V.wait_ge(sem["cv%d" % c], 1)
-        for bp in range(8):
-            i0 = c * CS + 32 * bp
-            V.transpose(T.yt[:, c * CS + bp:(c + 1) * CS:8], T.xb[:, i0:i0 + 32]).then_inc(sem["tr%d" % c], 1)
-
-    def masks(lo, hi):
-        for u in range(lo, hi):
-            V.tensor_scalar(T.lm[:, 128 * u:128 * u + 128], T.ident[:], T.k16[:, u:u + 1], None, OP.mult).then_inc(sem.vlm, 1)
+    def onehot_wires(l):
+        for i in range(2):
+            k = 2 * l + i
+            V.tensor_scalar(T.vt[:, 256 * k:256 * k + 256], T.iotl[:], T.wf[:, k:k + 1], 64.0 if i == 0 else 1.0,
+                            OP.is_equal, OP.mult).then_inc(sem["vvt%d" % l], 1)
 
     def onehot_give(l):
         for k in (2 * l, 2 * l + 1):
             V.tensor_scalar(T.gt[:, 128 * k:128 * k + 128], T.iotn[:], T.giv[:, k:k + 1], None, OP.is_equal).then_inc(sem["vgt%d" % l], 1)
 
+    def masks_s(lo, hi):
+        for u in range(lo, hi):
+            S.activation(T.lm[:, 128 * u:128 * u + 128], T.ident[:], ACT.Copy, scale=T.k16[:, u:u + 1]).then_inc(sem.slm, 1)
+
     def fix(c):
-        P.wait_ge(sem["tr%d" % c], 8)
+        P.wait_ge(sem["tr%d" % min(c, 2)], 1 if c else 8)
         if c == 0:
             P.wait_ge(sem.vpm, 4)
         if c >= 2:
             P.wait_ge(sem["ce%d" % (c - 2)], 1)
         for h in range(2):
-            for g2 in range(2):
-                k = 2 * g2 + h
-                m = P.matmul(psf[c % 2][:, 128 * h:128 * h + 128], T.pm[:, 128 * k:128 * k + 128],
-                             T.yt[:, c * CS + 128 * g2:c * CS + 128 * g2 + 128], g2 == 0, g2 == 1)
-                if g2 == 1:
-                    m.then_inc(sem["pf%d" % c], 1)
+            for bp in range(8 if c else 1):
+                for g2 in range(2):
+                    k = 2 * g2 + h
+                    if c:
+                        i0 = c * CS + 32 * bp + 16 * g2
+                        o, i = psf[c % 2][:, 128 * h + bp:128 * h + 128:8], T.yt[:, i0:i0 + 16]
+                    else:
+                        o, i = psf[0][:, 128 * h:128 * h + 128], T.yt[:, 128 * g2:128 * g2 + 128]
+                    m = P.matmul(o, T.pm[:, 128 * k:128 * k + 128], i, g2 == 0, g2 == 1)
+            m.then_inc(sem["pf%d" % c], 1)
 
     def compose_v(l):
         P.wait_ge(sem["vvt%d" % l], 2)
         for kh in range(2):
             for i in range(2):
                 a = (2 * l + i) * 256 + 128 * kh
-                m = P.matmul(T.psv[:, l * 256 + 128 * kh:l * 256 + 128 * kh + 128], T.vt[:, a:a + 128], T.ident[:], i == 0, i == 1)
+                m = P.matmul(psv[l][:, 128 * kh:128 * kh + 128], T.vt[:, a:a + 128], T.ident[:], i == 0, i == 1)
                 if i == 1:
                     m.then_inc(sem["pv%d" % l], 1)
 
@@ -158,13 +165,14 @@ def rank_program(g, core, T, topo):
                 m = P.matmul(psw[l][q][:, a:a + 128],
                              T.gt[32 * q:32 * q + 32, (2 * l + kh) * 128:(2 * l + kh) * 128 + 128],
                              T.vb[32 * q:32 * q + 32, l * 256 + 128 * kh:l * 256 + 128 * kh + 128], kh == 0, kh == 1)
-            m.then_inc(sem["pw1" if l else ("pwv" if q < 2 else "pws")], 1)
+            m.then_inc(sem["pw1" if l else ("pwv" if q < 3 else "pws")], 1)
 
     def addresses(l, c):
         if c == 0:
             if l == 0:
-                P.wait_ge(sem.swv, 2)
-                P.wait_ge(sem.sws, 2)
+                P.wait_ge(sem.swv, 3)
+                P.wait_ge(sem.sws, 1)
+                P.wait_ge(sem.sv1, 1)
             else:
                 P.wait_ge(sem.sw1, 1)
         P.wait_ge(sem["%s%d" % ("ce" if l == 0 else "sc", c)], 1)
@@ -177,21 +185,33 @@ def rank_program(g, core, T, topo):
                          cb[l][:, q * 1024 + c * CS:q * 1024 + (c + 1) * CS], q == 0, q == 3)
         m.then_inc(sem["pa%d%d" % (l, c)], 1)
 
+    def gpos(l, c, h):
+        if l == 0 or c < NCH - 1:
+            o, n = c * CS + h * TS, TS
+        else:
+            o, n = (NCH - 1) * CS + h * TS + (c - NCH + 1) * (TS // 2), TS // 2
+        return 16 * o, 16 * (o + n)
+
     def pick(l, c):
         if c == 0:
-            P.wait_ge(sem.vrm if l else sem.vlm, 1 if l else 16)
+            if l:
+                P.wait_ge(sem.vrm, 1)
+            else:
+                P.wait_ge(sem.vlm, 16 - SM)
+                P.wait_ge(sem.slm, SM)
         k = l * NCH + c - 2
         if k >= 0:
             P.wait_ge(sem["%s%d" % ("sc" if k < NCH else "sy", k % NCH)], 1)
         for h in range(2):
-            P.wait_ge(sem["%s%d%d" % ("gv" if h == 0 else "gsc", l, c)], 1)
-            j0 = (2 * c + h) * 2048
+            P.wait_ge(sem["%s%d%d" % ("gs" if h else "gv", l, c)], 1)
+            j0, j1 = gpos(l, c, h)
+            n = (j1 - j0) // 16
             for u in range(16):
-                src = ga[l][:, j0 + u:j0 + 2048:16]
+                src = ga[l][:, j0 + u:j1:16]
                 if l == 0:
                     m = P.matmul(psc[c % 2][:, 128 * h:128 * h + 128], T.lm[:, 128 * u:128 * u + 128], src, u == 0, u == 15)
                 else:
-                    m = P.matmul(psc[c % 2][:, 16 * h + u:256:32], src, T.rm[:, 8 * u:8 * u + 8], True, True)
+                    m = P.matmul(psc[c % 2][0:n, 16 * h + u:256:32], src, T.rm[:, 8 * u:8 * u + 8], True, True)
             m.then_inc(sem["pd%d%d" % (l, c)], 1)
 
     def evac_addr(l, c):
@@ -200,63 +220,79 @@ def rank_program(g, core, T, topo):
 
     def gather(l, c, h):
         q = S if h else V
-        q.wait_ge(sem["ea%d%d" % (l, c)], 1)
+        q.wait_ge(sem["ea%d%d" % (l, min(c, NCH - 1))], 1)
         if c == 0:
             q.wait_ge(sem["dt%d" % l], 16)
-        j0 = (2 * c + h) * 2048
-        o0 = c * CS + h * TS
-        win = tab[l][:, 0:4096].indirect(off[l][:, o0:o0 + TS])
+        j0, j1 = gpos(l, c, h)
+        win = tab[l][:, 0:4096].indirect(off[l][:, j0 // 16:j1 // 16])
         if h == 0:
-            V.tensor_copy(ga[l][:, j0:j0 + 2048], win).then_inc(sem["gv%d%d" % (l, c)], 1)
+            V.tensor_copy(ga[l][:, j0:j1], win).then_inc(sem["gv%d%d" % (l, c)], 1)
         else:
-            S.activation(ga[l][:, j0:j0 + 2048], win, ACT.Copy).then_inc(sem["gsc%d%d" % (l, c)], 1)
+            S.activation(ga[l][:, j0:j1], win, ACT.Copy).then_inc(sem["gs%d%d" % (l, c)], 1)
 
     def s_c0(c):
         S.wait_ge(sem["pf%d" % c], 2)
         S.activation(T.c0[:, own + c * CS:own + (c + 1) * CS], psf[c % 2][:, 0:CS], ACT.Copy).then_inc(sem["ce%d" % c], 1)
 
-    def s_out(l, c):
-        S.wait_ge(sem["pd%d%d" % (l, c)], 2)
-        dst = T.ys[:, c * CS:(c + 1) * CS] if l else T.c1[:, own + c * CS:own + (c + 1) * CS]
-        S.activation(dst, psc[c % 2][:, 0:CS], ACT.Copy).then_inc(sem["%s%d" % ("sy" if l else "sc", c)], 1)
+    def s_c1(c):
+        S.wait_ge(sem["pd0%d" % c], 2)
+        S.activation(T.c1[:, own + c * CS:own + (c + 1) * CS], psc[c % 2][:, 0:CS], ACT.Copy).then_inc(sem["sc%d" % c], 1)
 
-    V.wait_ge(sem.io1, 3)
+    def ysrc(c):
+        if c < NCH - 1:
+            return T.ys, c * CS, 128
+        return (T.ys, (NCH - 1) * CS, 64) if c == NCH - 1 else (T.yl, 0, 64)
+
+    def out_y(q, c):
+        q.wait_ge(sem["pd1%d" % c], 2)
+        b, a, n = ysrc(c)
+        if q is V:
+            m = V.tensor_copy(b[0:n, a:a + CS], psc[c % 2][0:n, 0:CS])
+        else:
+            m = S.activation(b[0:n, a:a + CS], psc[c % 2][0:n, 0:CS], ACT.Copy)
+        m.then_inc(sem["sy%d" % c], 1)
+
+    V.wait_ge(sem.iop, 2)
     V.tensor_scalar(T.pmi[:], T.pcol[:], 15, None, OP.bitwise_and).then_inc(sem.vi, 1)
     V.tensor_scalar(T.kbi[:], T.pcol[:], 4, 1, OP.logical_shift_right, OP.bitwise_and).then_inc(sem.vi, 1)
-    V.tensor_scalar(T.ident[:], T.diff[:], 0.0, None, OP.is_equal).then_inc(sem.vid, 1)
     V.wait_ge(sem.vi, 2)
     V.tensor_copy(T.pmf[:], T.pmi[:]).then_inc(sem.vf, 1)
     V.tensor_copy(T.kbf[:, 1:2], T.kbi[:]).then_inc(sem.vf, 1)
     V.tensor_scalar(T.kbf[:, 0:1], T.kbi[:], -1.0, 1.0, OP.mult, OP.add).then_inc(sem.vf, 1)
     V.wait_ge(sem.vf, 3)
+    V.tensor_scalar(T.k16[:], T.col16[:], T.pmf[:], None, OP.is_equal).then_inc(sem.vk, 1)
+    V.wait_ge(sem.iod, 1)
+    V.tensor_scalar(T.ident[:], T.diff[:], 0.0, None, OP.is_equal).then_inc(sem.vid, 1)
     for g2 in range(2):
         for h in range(2):
             k = 2 * g2 + h
             V.tensor_scalar(T.pm[:, 128 * k:128 * k + 128], T.diff[:], float(16 * (g2 - h)), T.kbf[:, h:h + 1],
                             OP.is_equal, OP.mult).then_inc(sem.vpm, 1)
-    V.tensor_scalar(T.k16[:], T.col16[:], T.pmf[:], None, OP.is_equal).then_inc(sem.vk, 1)
-    V.wait_ge(sem.io2, 3)
-    V.tensor_scalar(T.rm[:], T.rdiff[:], 0.0, None, OP.is_equal).then_inc(sem.vrm, 1)
+    V.wait_ge(sem.dx0, 16)
+    V.tensor_copy(T.xb[:, 0:CS], T.xi[:, 0:CS]).then_inc(sem.cv0, 1)
+    V.wait_ge(sem.cv0, 1)
+    for bp in range(8):
+        V.transpose(T.yt[:, bp:CS:8], T.xb[:, 32 * bp:32 * bp + 32]).then_inc(sem.tr0, 1)
     V.wait_ge(sem.dwr, 16)
     V.tensor_copy(T.wf[:], T.wi[:]).then_inc(sem.vwf, 1)
+    V.wait_ge(sem.iol, 1)
     V.wait_ge(sem.vwf, 1)
-    for l in range(2):
-        for i in range(2):
-            k = 2 * l + i
-            V.tensor_scalar(T.vt[:, 256 * k:256 * k + 256], T.iotl[:], T.wf[:, k:k + 1], 64.0 if i == 0 else 1.0,
-                            OP.is_equal, OP.mult).then_inc(sem["vvt%d" % l], 1)
-    V.wait_ge(sem.dx0, 16)
-    convert(0)
-    turn(0)
-    V.wait_ge(sem.vk, 1)
-    V.wait_ge(sem.vid, 1)
-    masks(0, 8)
+    onehot_wires(0)
     V.wait_ge(sem.pf0, 2)
     V.tensor_copy(T.c0[:, own:own + CS], T.psf0[:, 0:CS]).then_inc(sem.ce0, 1)
-    masks(8, 16)
     V.wait_ge(sem.dxr, 16)
-    for c in range(1, NCH):
-        convert(c)
+    V.tensor_copy(T.xb[:, CS:2 * CS], T.xi[:, CS:2 * CS]).then_inc(sem.cv1, 1)
+    V.tensor_copy(T.xb[:, 2 * CS:1024], T.xi[:, 2 * CS:1024]).then_inc(sem.cv2, 1)
+    V.wait_ge(sem.cv1, 1)
+    V.transpose(T.yt[:, CS:2 * CS], T.xb[:, CS:2 * CS]).then_inc(sem.tr1, 1)
+    onehot_wires(1)
+    V.wait_ge(sem.cv2, 1)
+    V.transpose(T.yt[:, 2 * CS:1024], T.xb[:, 2 * CS:1024]).then_inc(sem.tr2, 1)
+    V.wait_ge(sem.vk, 1)
+    V.wait_ge(sem.vid, 1)
+    for u in range(SM, 16):
+        V.tensor_scalar(T.lm[:, 128 * u:128 * u + 128], T.ident[:], T.k16[:, u:u + 1], None, OP.mult).then_inc(sem.vlm, 1)
+    V.wait_ge(sem.ion, 1)
     V.wait_ge(sem.dgv, 16)
     V.wait_ge(sem.agv, ne * n_oth)
     for q in range(4):
@@ -265,58 +301,64 @@ def rank_program(g, core, T, topo):
         V.tensor_copy(T.giv[32 * q:32 * q + 32, 0:4], src).then_inc(sem.vgiv, 1)
     V.wait_ge(sem.vgiv, 4)
     onehot_give(0)
-    turn(1)
-    V.wait_ge(sem.pwv, 2)
-    for q in range(2):
+    V.wait_ge(sem.pwv, 3)
+    for q in range(3):
         V.tensor_copy(T.w[:, 128 * q:128 * q + 128], psw[0][q][:, 0:128]).then_inc(sem.swv, 1)
-    turn(2)
     onehot_give(1)
-    turn(3)
+    V.wait_ge(sem.ior, 1)
+    V.tensor_scalar(T.rm[:], T.rdiff[:], 0.0, None, OP.is_equal).then_inc(sem.vrm, 1)
     for l in range(2):
         for c in range(NCH):
             evac_addr(l, c)
             gather(l, c, 0)
+            if l and c >= 2:
+                out_y(V, c - 1)
+    gather(1, 4, 0)
+    out_y(V, 3)
 
+    S.wait_ge(sem.vk, 1)
+    S.wait_ge(sem.vid, 1)
+    masks_s(0, 7)
     S.wait_ge(sem.pv0, 2)
-    S.wait_ge(sem.pv1, 2)
-    for l in range(2):
-        S.activation(T.vb[:, 256 * l:256 * l + 256], T.psv[:, 256 * l:256 * l + 256], ACT.Copy).then_inc(sem["sv%d" % l], 1)
-    S.wait_ge(sem.pws, 2)
-    for q in (2, 3):
-        S.activation(T.w[:, 128 * q:128 * q + 128], psw[0][q][:, 0:128], ACT.Copy).then_inc(sem.sws, 1)
+    S.activation(T.vb[:, 0:256], psv[0][:, 0:256], ACT.Copy).then_inc(sem.sv0, 1)
+    masks_s(7, 10)
     s_c0(1)
+    S.wait_ge(sem.pv1, 2)
+    S.activation(T.vb[:, 256:512], psv[1][:, 0:256], ACT.Copy).then_inc(sem.sv1, 1)
+    S.wait_ge(sem.pws, 1)
+    S.activation(T.w[:, 384:512], psw[0][3][:, 0:128], ACT.Copy).then_inc(sem.sws, 1)
+    masks_s(10, SM)
     s_c0(2)
     gather(0, 0, 1)
     s_c0(3)
     gather(0, 1, 1)
     S.wait_ge(sem.pw1, 4)
     S.activation(T.w[:, 512:1024], T.psw[:], ACT.Copy).then_inc(sem.sw1, 1)
-    s_out(0, 0)
+    s_c1(0)
     gather(0, 2, 1)
-    s_out(0, 1)
+    s_c1(1)
     gather(0, 3, 1)
-    s_out(0, 2)
+    s_c1(2)
     gather(1, 0, 1)
-    s_out(0, 3)
+    s_c1(3)
     gather(1, 1, 1)
-    s_out(1, 0)
+    out_y(S, 0)
     gather(1, 2, 1)
-    s_out(1, 1)
     gather(1, 3, 1)
-    s_out(1, 2)
-    s_out(1, 3)
+    gather(1, 4, 1)
+    out_y(S, 4)
 
     P.wait_ge(sem.vid, 1)
-    compose_v(0)
-    compose_v(1)
     fix(0)
-    compose_w(0)
+    compose_v(0)
     fix(1)
+    compose_v(1)
+    compose_w(0)
     fix(2)
     addresses(0, 0)
     fix(3)
-    compose_w(1)
     addresses(0, 1)
+    compose_w(1)
     pick(0, 0)
     addresses(0, 2)
     pick(0, 1)
@@ -331,15 +373,19 @@ def rank_program(g, core, T, topo):
     addresses(1, 3)
     pick(1, 2)
     pick(1, 3)
+    pick(1, 4)
 
     Y.wait_ge(sem.ea00, 1)
     Y.dma_start(T.tab1[:], T.tb[:, 65536:131072]).then_inc(sem.dt1, 16)
-    for c in range(NCH):
-        last = c == NCH - 1
+    for c in range(NCH + 1):
+        last = c == NCH
         Y.wait_ge(sem["sy%d" % c], 1)
         if last:
             S.wait_ge(sem["sy%d" % c], 1)
+        b, a, n = ysrc(c)
+        cc = min(c, NCH - 1)
         for gg in range(8):
             q = S if last and gg % 2 else Y
-            q.dma_start(T.y[16 * gg:16 * gg + 16, c * CS:(c + 1) * CS], T.ys[:, c * CS + 32 * gg:c * CS + 32 * gg + 32]).then_inc(sem.dy, 16)
-    Y.wait_ge(sem.dy, 16 * 8 * NCH)
+            r0 = 16 * gg + (8 if last else 0)
+            q.dma_start(T.y[r0:r0 + n // 8, cc * CS:(cc + 1) * CS], b[0:n, a + 32 * gg:a + 32 * gg + 32]).then_inc(sem.dy, 16)
+    Y.wait_ge(sem.dy, 16 * 8 * (NCH + 1))

@@ -3,8 +3,8 @@ from concourse.mybir import AluOpType as OP, ActivationFunctionType as ACT
 
 NCH = 4
 CS = 256
-TS = 128
-SM = 12
+SPL = [[124, 132, 126, 126], [122, 122, 128, 0]]
+SA = 11
 
 SCRATCH = {
     "xi": ("sbuf", [128, 1024], "int32"),
@@ -16,14 +16,10 @@ SCRATCH = {
     "wi": ("sbuf", [128, 4], "int32"),
     "wf": ("sbuf", [128, 4], "float32"),
     "pcol": ("sbuf", [128, 1], "int32"),
-    "pmi": ("sbuf", [128, 1], "int32"),
     "kbi": ("sbuf", [128, 1], "int32"),
-    "pmf": ("sbuf", [128, 1], "float32"),
     "kbf": ("sbuf", [128, 2], "float32"),
-    "col16": ("sbuf", [128, 16], "float32"),
-    "k16": ("sbuf", [128, 16], "float32"),
-    "diff": ("sbuf", [128, 128], "float32"),
-    "rdiff": ("sbuf", [128, 128], "float32"),
+    "ones": ("sbuf", [128, 512], "bfloat16"),
+    "diff": ("sbuf", [128, 128], "bfloat16"),
     "iotn": ("sbuf", [128, 128], "bfloat16"),
     "iotl": ("sbuf", [128, 256], "bfloat16"),
     "ident": ("sbuf", [128, 128], "bfloat16"),
@@ -53,8 +49,8 @@ SCRATCH = {
     "psc0": ("psum", [128, 512], "float32"),
     "psc1": ("psum", [128, 512], "float32"),
 }
-SEMAPHORES = (["dx0", "dxr", "dgv", "dwr", "dt0", "dt1", "dy", "iop", "iod", "iol", "ion", "ior", "vi", "vf", "vk", "vid",
-               "vpm", "vlm", "slm", "vrm", "vwf", "vvt0", "vvt1", "vgiv", "vgt0", "vgt1", "pv0", "pv1", "sv0", "sv1",
+SEMAPHORES = (["dx0", "dxr", "dgv", "dwr", "dt0", "dt1", "dy", "iop", "iod", "iol", "ion", "von", "lmg", "rmg",
+               "vi", "vf", "vid", "vpm", "vwf", "vvt0", "vvt1", "vgiv", "vgt0", "vgt1", "pv0", "pv1", "sv0", "sv1",
                "pwv", "pws", "pw1", "swv", "sws", "sw1", "agv", "loc", "cv0", "cv1", "cv2", "tr0", "tr1", "tr2"]
               + ["%s%d" % (a, c) for c in range(NCH) for a in ("pf", "ce", "ac", "bc", "sc")]
               + ["%s%d%d" % (a, l, c) for l in range(2) for c in range(NCH) for a in ("pa", "ea")]
@@ -90,50 +86,61 @@ def rank_program(g, core, T, topo):
     psw = [[T.psc0, T.psc1, T.psw, T.psa1], [T.psw] * 4]
     psv = [T.psv, T.psa0]
 
-    Y.dma_start(T.xi[:, 0:CS], T.x[:, 0:CS]).then_inc(sem.dx0, 16)
     S.dma_start(T.gs[:], T.give[:]).then_inc(sem.dgv, 16)
+    Y.dma_start(T.xi[:, 0:CS], T.x[:, 0:CS]).then_inc(sem.dx0, 16)
     S.dma_start(T.wi[:], T.wires[:]).then_inc(sem.dwr, 16)
     Y.dma_start(T.xi[:, CS:1024], T.x[:, CS:1024]).then_inc(sem.dxr, 16)
-    Y.dma_start(T.tab0[:], T.tb[:, 0:65536]).then_inc(sem.dt0, 16)
+    Y.dma_start(T.tab0[0:64, :], T.tb[0:4, 0:65536]).then_inc(sem.dt0, 16)
+    Y.wait_ge(sem.dxr, 16)
+    Y.dma_start(T.tab0[64:128, :], T.tb[4:8, 0:65536]).then_inc(sem.dt0, 16)
 
     lax = {"allow_small_or_imprecise_dtypes": True}
     g.iota(T.pcol[:], [[1, 1]], 0, 1).then_inc(sem.iop, 1)
-    g.iota(T.col16[:], [[1, 16]], 0, 0, **lax).then_inc(sem.iop, 1)
     g.iota(T.diff[:], [[1, 128]], 0, -1, **lax).then_inc(sem.iod, 1)
     g.iota(T.iotl[:], [[16, 2], [32, 8], [1, 16]], 0, 0, **lax).then_inc(sem.iol, 1)
+    g.iota(T.iotn[:], [[1, 128]], 0, 0, **lax).then_inc(sem.ion, 1)
+
+    def masks(i):
+        g.affine_select(T.lm[:, 512 * i:512 * i + 512], T.ones[:], [[1000, 4], [-16, 8], [-1001, 16]], OP.is_equal, 0.0,
+                        4000 * i, 1).then_inc(sem.lmg, 1)
+
+    def send(l, c):
+        g.wait_ge(sem["%s%d" % ("sc" if l else "ce", c)], 1)
+        a = own + c * CS
+        bcast(cb[l][:, a:a + CS], cb[l][:, a:a + CS], "%s%d" % ("bc" if l else "ac", c))
+
     g.wait_ge(sem.dgv, 16)
     bcast(T.gs[:], T.gl[:, 4 * rank:4 * rank + 4], "agv")
-    g.iota(T.iotn[:], [[1, 128]], 0, 0, **lax).then_inc(sem.ion, 1)
-    for l in range(2):
-        for c in range(NCH):
-            g.wait_ge(sem["%s%d" % ("sc" if l else "ce", c)], 1)
-            a = own + c * CS
-            bcast(cb[l][:, a:a + CS], cb[l][:, a:a + CS], "%s%d" % ("bc" if l else "ac", c))
-            if l == 0 and c == 0:
-                g.iota(T.rdiff[:], [[1, 16], [16, 8]], 0, -1, **lax).then_inc(sem.ior, 1)
+    send(0, 0)
+    g.wait_ge(sem.von, 1)
+    masks(0)
+    send(0, 1)
+    masks(1)
+    send(0, 2)
+    masks(2)
+    masks(3)
+    send(0, 3)
+    g.affine_select(T.rm[:], T.ones[:, 0:128], [[-1, 16], [-16, 8]], OP.is_equal, 0.0, 0, 1).then_inc(sem.rmg, 1)
+    for c in range(NCH):
+        send(1, c)
     g.wait_ge(sem.loc, ne * (1 + 2 * NCH))
 
-    def onehot_wires(l):
-        for i in range(2):
-            k = 2 * l + i
-            V.tensor_scalar(T.vt[:, 256 * k:256 * k + 256], T.iotl[:], T.wf[:, k:k + 1], 64.0 if i == 0 else 1.0,
-                            OP.is_equal, OP.mult).then_inc(sem["vvt%d" % l], 1)
+    def onehot_wires(l, i):
+        k = 2 * l + i
+        V.tensor_scalar(T.vt[:, 256 * k:256 * k + 256], T.iotl[:], T.wf[:, k:k + 1], 64.0 if i == 0 else 1.0,
+                        OP.is_equal, OP.mult).then_inc(sem["vvt%d" % l], 1)
 
     def onehot_give(l):
         for k in (2 * l, 2 * l + 1):
             V.tensor_scalar(T.gt[:, 128 * k:128 * k + 128], T.iotn[:], T.giv[:, k:k + 1], None, OP.is_equal).then_inc(sem["vgt%d" % l], 1)
 
-    def masks_s(lo, hi):
-        for u in range(lo, hi):
-            S.activation(T.lm[:, 128 * u:128 * u + 128], T.ident[:], ACT.Copy, scale=T.k16[:, u:u + 1]).then_inc(sem.slm, 1)
-
-    def fix(c):
+    def fix(c, halves=(0, 1)):
         P.wait_ge(sem["tr%d" % min(c, 2)], 1 if c else 8)
         if c == 0:
             P.wait_ge(sem.vpm, 4)
         if c >= 2:
             P.wait_ge(sem["ce%d" % (c - 2)], 1)
-        for h in range(2):
+        for h in halves:
             for bp in range(8 if c else 1):
                 for g2 in range(2):
                     k = 2 * g2 + h
@@ -154,81 +161,93 @@ def rank_program(g, core, T, topo):
                 if i == 1:
                     m.then_inc(sem["pv%d" % l], 1)
 
-    def compose_w(l):
-        P.wait_ge(sem["vgt%d" % l], 2)
-        P.wait_ge(sem["sv%d" % l], 1)
+    def w_part(l, q, kh):
+        a = 128 * q if l else 0
+        return P.matmul(psw[l][q][:, a:a + 128],
+                        T.gt[32 * q:32 * q + 32, (2 * l + kh) * 128:(2 * l + kh) * 128 + 128],
+                        T.vb[32 * q:32 * q + 32, l * 256 + 128 * kh:l * 256 + 128 * kh + 128], kh == 0, kh == 1)
+
+    def compose_w0():
+        P.wait_ge(sem.sv0, 1)
+        for kh in range(2):
+            P.wait_ge(sem.vgt0, kh + 1)
+            for q in range(4):
+                m = w_part(0, q, kh)
+                if kh:
+                    m.then_inc(sem["pwv" if q < 3 else "pws"], 1)
+
+    def compose_w1():
+        P.wait_ge(sem.vgt1, 2)
+        P.wait_ge(sem.sv1, 1)
         for q in range(4):
-            if l and q:
+            if q:
                 P.wait_ge(sem.pw1, q)
-            a = 128 * q if l else 0
-            for kh in range(2):
-                m = P.matmul(psw[l][q][:, a:a + 128],
-                             T.gt[32 * q:32 * q + 32, (2 * l + kh) * 128:(2 * l + kh) * 128 + 128],
-                             T.vb[32 * q:32 * q + 32, l * 256 + 128 * kh:l * 256 + 128 * kh + 128], kh == 0, kh == 1)
-            m.then_inc(sem["pw1" if l else ("pwv" if q < 3 else "pws")], 1)
+            w_part(1, q, 0)
+            w_part(1, q, 1).then_inc(sem.pw1, 1)
 
     def addresses(l, c):
-        if c == 0:
-            if l == 0:
-                P.wait_ge(sem.swv, 3)
-                P.wait_ge(sem.sws, 1)
-                P.wait_ge(sem.sv1, 1)
-            else:
-                P.wait_ge(sem.sw1, 1)
         P.wait_ge(sem["%s%d" % ("ce" if l == 0 else "sc", c)], 1)
         P.wait_ge(sem["%s%d" % ("ac" if l == 0 else "bc", c)], ne * n_oth)
+        if c == 0:
+            P.wait_ge(sem.sw1 if l else sem.sv1, 1)
         k = l * NCH + c - 2
         if k >= 0:
-            P.wait_ge(sem["ea%d%d" % (k // NCH, k % NCH)], 1)
+            P.wait_ge(sem["ea%d%d" % (k // NCH, k % NCH)], 2)
         for q in range(4):
+            if l == 0 and c == 0:
+                P.wait_ge(sem.swv if q < 3 else sem.sws, q + 1 if q < 3 else 1)
             m = P.matmul(psa[c % 2][:, 0:CS], T.w[:, (4 * l + q) * 128:(4 * l + q) * 128 + 128],
                          cb[l][:, q * 1024 + c * CS:q * 1024 + (c + 1) * CS], q == 0, q == 3)
         m.then_inc(sem["pa%d%d" % (l, c)], 1)
 
     def gpos(l, c, h):
         if l == 0 or c < NCH - 1:
-            o, n = c * CS + h * TS, TS
-        else:
-            o, n = (NCH - 1) * CS + h * TS + (c - NCH + 1) * (TS // 2), TS // 2
-        return 16 * o, 16 * (o + n)
+            nv = SPL[l][c]
+            return (c * CS + nv, (c + 1) * CS) if h else (c * CS, c * CS + nv)
+        o = (NCH - 1) * CS + 128 * h
+        return (o, o + 8 * SA) if c == NCH - 1 else (o + 8 * SA, o + 128)
+
+    def tile(c, h):
+        return gpos(1, c, h) if c >= NCH - 1 else (c * CS + 128 * h, c * CS + 128 * h + 128)
 
     def pick(l, c):
         if c == 0:
             if l:
-                P.wait_ge(sem.vrm, 1)
+                P.wait_ge(sem.rmg, 1)
             else:
-                P.wait_ge(sem.vlm, 16 - SM)
-                P.wait_ge(sem.slm, SM)
+                P.wait_ge(sem.lmg, 4)
         k = l * NCH + c - 2
         if k >= 0:
             P.wait_ge(sem["%s%d" % ("sc" if k < NCH else "sy", k % NCH)], 1)
         for h in range(2):
             P.wait_ge(sem["%s%d%d" % ("gs" if h else "gv", l, c)], 1)
-            j0, j1 = gpos(l, c, h)
-            n = (j1 - j0) // 16
+            j0, j1 = tile(c, h) if l else gpos(0, c, h)
+            if l and h == 0 and j1 > gpos(1, c, 0)[1]:
+                P.wait_ge(sem["gs%d%d" % (l, c)], 1)
             for u in range(16):
-                src = ga[l][:, j0 + u:j1:16]
+                src = ga[l][:, 16 * j0 + u:16 * j1:16]
                 if l == 0:
-                    m = P.matmul(psc[c % 2][:, 128 * h:128 * h + 128], T.lm[:, 128 * u:128 * u + 128], src, u == 0, u == 15)
+                    m = P.matmul(psc[c % 2][:, j0 - c * CS:j1 - c * CS], T.lm[:, 128 * u:128 * u + 128], src, u == 0, u == 15)
                 else:
-                    m = P.matmul(psc[c % 2][0:n, 16 * h + u:256:32], src, T.rm[:, 8 * u:8 * u + 8], True, True)
+                    m = P.matmul(psc[c % 2][0:j1 - j0, 16 * h + u:256:32], src, T.rm[:, 8 * u:8 * u + 8], True, True)
             m.then_inc(sem["pd%d%d" % (l, c)], 1)
 
     def evac_addr(l, c):
         V.wait_ge(sem["pa%d%d" % (l, c)], 1)
-        V.tensor_copy(off[l][:, c * CS:(c + 1) * CS], psa[c % 2][:, 0:CS]).then_inc(sem["ea%d%d" % (l, c)], 1)
+        for a, b in (gpos(l, c, 0), gpos(l, c, 1)) if SPL[l][c] else ((c * CS, (c + 1) * CS),):
+            V.tensor_copy(off[l][:, a:b], psa[c % 2][:, a - c * CS:b - c * CS]).then_inc(sem["ea%d%d" % (l, c)], 1)
 
     def gather(l, c, h):
         q = S if h else V
-        q.wait_ge(sem["ea%d%d" % (l, min(c, NCH - 1))], 1)
+        q.wait_ge(sem["ea%d%d" % (l, min(c, NCH - 1))], 2 if h and SPL[l][min(c, NCH - 1)] else 1)
         if c == 0:
-            q.wait_ge(sem["dt%d" % l], 16)
+            q.wait_ge(sem["dt%d" % l], 16 if l else 32)
         j0, j1 = gpos(l, c, h)
-        win = tab[l][:, 0:4096].indirect(off[l][:, j0 // 16:j1 // 16])
+        win = tab[l][:, 0:4096].indirect(off[l][:, j0:j1])
         if h == 0:
-            V.tensor_copy(ga[l][:, j0:j1], win).then_inc(sem["gv%d%d" % (l, c)], 1)
+            V.tensor_copy(ga[l][:, 16 * j0:16 * j1], win).then_inc(sem["gv%d%d" % (l, c)], 1)
         else:
-            S.activation(ga[l][:, j0:j1], win, ACT.Copy).then_inc(sem["gs%d%d" % (l, c)], 1)
+            S.activation(ga[l][:, 16 * j0:16 * j1], win, ACT.Copy).then_inc(sem["gs%d%d" % (l, c)], 1)
 
     def s_c0(c):
         S.wait_ge(sem["pf%d" % c], 2)
@@ -241,7 +260,7 @@ def rank_program(g, core, T, topo):
     def ysrc(c):
         if c < NCH - 1:
             return T.ys, c * CS, 128
-        return (T.ys, (NCH - 1) * CS, 64) if c == NCH - 1 else (T.yl, 0, 64)
+        return (T.ys, (NCH - 1) * CS, 8 * SA) if c == NCH - 1 else (T.yl, 0, 128 - 8 * SA)
 
     def out_y(q, c):
         q.wait_ge(sem["pd1%d" % c], 2)
@@ -252,46 +271,41 @@ def rank_program(g, core, T, topo):
             m = S.activation(b[0:n, a:a + CS], psc[c % 2][0:n, 0:CS], ACT.Copy)
         m.then_inc(sem["sy%d" % c], 1)
 
-    V.wait_ge(sem.iop, 2)
-    V.tensor_scalar(T.pmi[:], T.pcol[:], 15, None, OP.bitwise_and).then_inc(sem.vi, 1)
+    V.memset(T.ones[:], 1.0).then_inc(sem.von, 1)
+    V.wait_ge(sem.iop, 1)
     V.tensor_scalar(T.kbi[:], T.pcol[:], 4, 1, OP.logical_shift_right, OP.bitwise_and).then_inc(sem.vi, 1)
-    V.wait_ge(sem.vi, 2)
-    V.tensor_copy(T.pmf[:], T.pmi[:]).then_inc(sem.vf, 1)
+    V.wait_ge(sem.vi, 1)
     V.tensor_copy(T.kbf[:, 1:2], T.kbi[:]).then_inc(sem.vf, 1)
     V.tensor_scalar(T.kbf[:, 0:1], T.kbi[:], -1.0, 1.0, OP.mult, OP.add).then_inc(sem.vf, 1)
-    V.wait_ge(sem.vf, 3)
-    V.tensor_scalar(T.k16[:], T.col16[:], T.pmf[:], None, OP.is_equal).then_inc(sem.vk, 1)
     V.wait_ge(sem.iod, 1)
     V.tensor_scalar(T.ident[:], T.diff[:], 0.0, None, OP.is_equal).then_inc(sem.vid, 1)
+    V.wait_ge(sem.vf, 2)
     for g2 in range(2):
         for h in range(2):
             k = 2 * g2 + h
             V.tensor_scalar(T.pm[:, 128 * k:128 * k + 128], T.diff[:], float(16 * (g2 - h)), T.kbf[:, h:h + 1],
                             OP.is_equal, OP.mult).then_inc(sem.vpm, 1)
     V.wait_ge(sem.dx0, 16)
-    V.tensor_copy(T.xb[:, 0:CS], T.xi[:, 0:CS]).then_inc(sem.cv0, 1)
-    V.wait_ge(sem.cv0, 1)
-    for bp in range(8):
-        V.transpose(T.yt[:, bp:CS:8], T.xb[:, 32 * bp:32 * bp + 32]).then_inc(sem.tr0, 1)
+    for h in range(2):
+        V.tensor_copy(T.xb[:, 128 * h:128 * h + 128], T.xi[:, 128 * h:128 * h + 128]).then_inc(sem.cv0, 1)
     V.wait_ge(sem.dwr, 16)
     V.tensor_copy(T.wf[:], T.wi[:]).then_inc(sem.vwf, 1)
+    for bp in range(8):
+        V.wait_ge(sem.cv0, 1 + bp // 4)
+        V.transpose(T.yt[:, bp:CS:8], T.xb[:, 32 * bp:32 * bp + 32]).then_inc(sem.tr0, 1)
     V.wait_ge(sem.iol, 1)
     V.wait_ge(sem.vwf, 1)
-    onehot_wires(0)
-    V.wait_ge(sem.pf0, 2)
-    V.tensor_copy(T.c0[:, own:own + CS], T.psf0[:, 0:CS]).then_inc(sem.ce0, 1)
+    onehot_wires(0, 0)
     V.wait_ge(sem.dxr, 16)
     V.tensor_copy(T.xb[:, CS:2 * CS], T.xi[:, CS:2 * CS]).then_inc(sem.cv1, 1)
-    V.tensor_copy(T.xb[:, 2 * CS:1024], T.xi[:, 2 * CS:1024]).then_inc(sem.cv2, 1)
+    onehot_wires(0, 1)
     V.wait_ge(sem.cv1, 1)
     V.transpose(T.yt[:, CS:2 * CS], T.xb[:, CS:2 * CS]).then_inc(sem.tr1, 1)
-    onehot_wires(1)
+    V.tensor_copy(T.xb[:, 2 * CS:1024], T.xi[:, 2 * CS:1024]).then_inc(sem.cv2, 1)
+    onehot_wires(1, 0)
+    onehot_wires(1, 1)
     V.wait_ge(sem.cv2, 1)
     V.transpose(T.yt[:, 2 * CS:1024], T.xb[:, 2 * CS:1024]).then_inc(sem.tr2, 1)
-    V.wait_ge(sem.vk, 1)
-    V.wait_ge(sem.vid, 1)
-    for u in range(SM, 16):
-        V.tensor_scalar(T.lm[:, 128 * u:128 * u + 128], T.ident[:], T.k16[:, u:u + 1], None, OP.mult).then_inc(sem.vlm, 1)
     V.wait_ge(sem.ion, 1)
     V.wait_ge(sem.dgv, 16)
     V.wait_ge(sem.agv, ne * n_oth)
@@ -301,39 +315,37 @@ def rank_program(g, core, T, topo):
         V.tensor_copy(T.giv[32 * q:32 * q + 32, 0:4], src).then_inc(sem.vgiv, 1)
     V.wait_ge(sem.vgiv, 4)
     onehot_give(0)
-    V.wait_ge(sem.pwv, 3)
     for q in range(3):
+        V.wait_ge(sem.pwv, q + 1)
         V.tensor_copy(T.w[:, 128 * q:128 * q + 128], psw[0][q][:, 0:128]).then_inc(sem.swv, 1)
     onehot_give(1)
-    V.wait_ge(sem.ior, 1)
-    V.tensor_scalar(T.rm[:], T.rdiff[:], 0.0, None, OP.is_equal).then_inc(sem.vrm, 1)
-    for l in range(2):
-        for c in range(NCH):
-            evac_addr(l, c)
-            gather(l, c, 0)
-            if l and c >= 2:
-                out_y(V, c - 1)
+    for c in range(NCH):
+        evac_addr(0, c)
+        gather(0, c, 0)
+    for c in range(NCH):
+        evac_addr(1, c)
+        if c == NCH - 1:
+            out_y(V, 1)
+        gather(1, c, 0)
+    out_y(V, 2)
     gather(1, 4, 0)
     out_y(V, 3)
+    out_y(V, 4)
 
-    S.wait_ge(sem.vk, 1)
-    S.wait_ge(sem.vid, 1)
-    masks_s(0, 7)
+    s_c0(0)
     S.wait_ge(sem.pv0, 2)
     S.activation(T.vb[:, 0:256], psv[0][:, 0:256], ACT.Copy).then_inc(sem.sv0, 1)
-    masks_s(7, 10)
     s_c0(1)
     S.wait_ge(sem.pv1, 2)
     S.activation(T.vb[:, 256:512], psv[1][:, 0:256], ACT.Copy).then_inc(sem.sv1, 1)
     S.wait_ge(sem.pws, 1)
     S.activation(T.w[:, 384:512], psw[0][3][:, 0:128], ACT.Copy).then_inc(sem.sws, 1)
-    masks_s(10, SM)
     s_c0(2)
     gather(0, 0, 1)
     s_c0(3)
-    gather(0, 1, 1)
     S.wait_ge(sem.pw1, 4)
     S.activation(T.w[:, 512:1024], T.psw[:], ACT.Copy).then_inc(sem.sw1, 1)
+    gather(0, 1, 1)
     s_c1(0)
     gather(0, 2, 1)
     s_c1(1)
@@ -346,19 +358,19 @@ def rank_program(g, core, T, topo):
     gather(1, 2, 1)
     gather(1, 3, 1)
     gather(1, 4, 1)
-    out_y(S, 4)
 
     P.wait_ge(sem.vid, 1)
     fix(0)
     compose_v(0)
     fix(1)
     compose_v(1)
-    compose_w(0)
-    fix(2)
+    fix(2, (0,))
+    compose_w0()
+    fix(2, (1,))
     addresses(0, 0)
     fix(3)
+    compose_w1()
     addresses(0, 1)
-    compose_w(1)
     pick(0, 0)
     addresses(0, 2)
     pick(0, 1)
@@ -375,10 +387,10 @@ def rank_program(g, core, T, topo):
     pick(1, 3)
     pick(1, 4)
 
-    Y.wait_ge(sem.ea00, 1)
+    Y.wait_ge(sem.ea00, 2)
     Y.dma_start(T.tab1[:], T.tb[:, 65536:131072]).then_inc(sem.dt1, 16)
     for c in range(NCH + 1):
-        last = c == NCH
+        last = c >= NCH - 1
         Y.wait_ge(sem["sy%d" % c], 1)
         if last:
             S.wait_ge(sem["sy%d" % c], 1)
@@ -386,6 +398,6 @@ def rank_program(g, core, T, topo):
         cc = min(c, NCH - 1)
         for gg in range(8):
             q = S if last and gg % 2 else Y
-            r0 = 16 * gg + (8 if last else 0)
+            r0 = 16 * gg + (SA if c == NCH else 0)
             q.dma_start(T.y[r0:r0 + n // 8, cc * CS:(cc + 1) * CS], b[0:n, a + 32 * gg:a + 32 * gg + 32]).then_inc(sem.dy, 16)
     Y.wait_ge(sem.dy, 16 * 8 * (NCH + 1))

from concourse.bass import DstId, RemoteDMATransfer
from concourse.mybir import AluOpType as OP, ActivationFunctionType as ACT

NCH = 4
CS = 256
SPL = [[124, 132, 126, 126], [122, 122, 128, 0]]
SA = 11

SCRATCH = {
    "xi": ("sbuf", [128, 1024], "int32"),
    "xb": ("sbuf", [128, 1024], "bfloat16"),
    "yt": ("sbuf", [128, 1024], "bfloat16"),
    "gs": ("sbuf", [128, 4], "int32"),
    "gl": ("sbuf", [128, 16], "int32"),
    "giv": ("sbuf", [128, 4], "float32"),
    "wi": ("sbuf", [128, 4], "int32"),
    "wf": ("sbuf", [128, 4], "float32"),
    "pcol": ("sbuf", [128, 1], "int32"),
    "kbi": ("sbuf", [128, 1], "int32"),
    "kbf": ("sbuf", [128, 2], "float32"),
    "ones": ("sbuf", [128, 512], "bfloat16"),
    "diff": ("sbuf", [128, 128], "bfloat16"),
    "iotn": ("sbuf", [128, 128], "bfloat16"),
    "iotl": ("sbuf", [128, 256], "bfloat16"),
    "ident": ("sbuf", [128, 128], "bfloat16"),
    "pm": ("sbuf", [128, 512], "bfloat16"),
    "lm": ("sbuf", [128, 2048], "bfloat16"),
    "rm": ("sbuf", [128, 128], "bfloat16"),
    "vt": ("sbuf", [128, 1024], "bfloat16"),
    "vb": ("sbuf", [128, 512], "bfloat16"),
    "gt": ("sbuf", [128, 512], "bfloat16"),
    "w": ("sbuf", [128, 1024], "bfloat16"),
    "c0": ("sbuf", [128, 4096], "bfloat16"),
    "c1": ("sbuf", [128, 4096], "bfloat16"),
    "tab0": ("sbuf", [128, 4096], "bfloat16"),
    "tab1": ("sbuf", [128, 4096], "bfloat16"),
    "off0": ("sbuf", [128, 1024], "uint16"),
    "off1": ("sbuf", [128, 1024], "uint16"),
    "ga0": ("sbuf", [128, 16384], "bfloat16"),
    "ga1": ("sbuf", [128, 16384], "bfloat16"),
    "ys": ("sbuf", [128, 1024], "float32"),
    "yl": ("sbuf", [128, 256], "float32"),
    "psv": ("psum", [128, 512], "float32"),
    "psw": ("psum", [128, 512], "float32"),
    "psf0": ("psum", [128, 512], "float32"),
    "psf1": ("psum", [128, 512], "float32"),
    "psa0": ("psum", [128, 512], "float32"),
    "psa1": ("psum", [128, 512], "float32"),
    "psc0": ("psum", [128, 512], "float32"),
    "psc1": ("psum", [128, 512], "float32"),
}
SEMAPHORES = (["dx0", "dxr", "dgv", "dwr", "dt0", "dt1", "dy", "iop", "iod", "iol", "ion", "von", "lmg", "rmg",
               "vi", "vf", "vid", "vpm", "vwf", "vvt0", "vvt1", "vgiv", "vgt0", "vgt1", "pv0", "pv1", "sv0", "sv1",
               "pwv", "pws", "pw1", "swv", "sws", "sw1", "agv", "loc", "cv0", "cv1", "cv2", "tr0", "tr1", "tr2"]
              + ["%s%d" % (a, c) for c in range(NCH) for a in ("pf", "ce", "ac", "bc", "sc")]
              + ["%s%d%d" % (a, l, c) for l in range(2) for c in range(NCH) for a in ("pa", "ea")]
              + ["%s%d%d" % (a, l, c) for l in range(2) for c in range(NCH + l) for a in ("gv", "gs", "pd")]
              + ["sy%d" % c for c in range(NCH + 1)])


def rank_program(g, core, T, topo):
    rank = T.rank_of(core)
    if rank is None:
        return
    V, S, P, Y = g.vector, g.scalar, g.tensor, g.sync
    sem = T.sem
    others = [c for c in T.cores if c != core]
    n_oth = len(others)
    engs = topo.engines(core, others[0])
    for c in others:
        engs = [e for e in engs if e in topo.engines(core, c)]
    ne = len(engs)
    emask = sum(1 << e for e in engs)
    ids = []
    for c in others:
        a = topo.addr(c)
        ids.append(DstId(rid=a[0], pnc=a[1]))

    def bcast(src, dst, name):
        g.remote_dma_fused([RemoteDMATransfer(dst_ids=ids, dma_engine_mask=emask, remote_sem=sem[name],
                                              srcs=[src], dsts=[dst] * n_oth)], local_sem=sem.loc)

    own = rank * 1024
    psf, psa, psc = [T.psf0, T.psf1], [T.psa0, T.psa1], [T.psc0, T.psc1]
    cb, tab, off, ga = [T.c0, T.c1], [T.tab0, T.tab1], [T.off0, T.off1], [T.ga0, T.ga1]
    psw = [[T.psc0, T.psc1, T.psw, T.psa1], [T.psw] * 4]
    psv = [T.psv, T.psa0]

    S.dma_start(T.gs[:], T.give[:]).then_inc(sem.dgv, 16)
    Y.dma_start(T.xi[:, 0:CS], T.x[:, 0:CS]).then_inc(sem.dx0, 16)
    S.dma_start(T.wi[:], T.wires[:]).then_inc(sem.dwr, 16)
    Y.dma_start(T.xi[:, CS:1024], T.x[:, CS:1024]).then_inc(sem.dxr, 16)
    Y.dma_start(T.tab0[0:64, :], T.tb[0:4, 0:65536]).then_inc(sem.dt0, 16)
    Y.wait_ge(sem.dxr, 16)
    Y.dma_start(T.tab0[64:128, :], T.tb[4:8, 0:65536]).then_inc(sem.dt0, 16)

    lax = {"allow_small_or_imprecise_dtypes": True}
    g.iota(T.pcol[:], [[1, 1]], 0, 1).then_inc(sem.iop, 1)
    g.iota(T.diff[:], [[1, 128]], 0, -1, **lax).then_inc(sem.iod, 1)
    g.iota(T.iotl[:], [[16, 2], [32, 8], [1, 16]], 0, 0, **lax).then_inc(sem.iol, 1)
    g.iota(T.iotn[:], [[1, 128]], 0, 0, **lax).then_inc(sem.ion, 1)

    def masks(i):
        g.affine_select(T.lm[:, 512 * i:512 * i + 512], T.ones[:], [[1000, 4], [-16, 8], [-1001, 16]], OP.is_equal, 0.0,
                        4000 * i, 1).then_inc(sem.lmg, 1)

    def send(l, c):
        g.wait_ge(sem["%s%d" % ("sc" if l else "ce", c)], 1)
        a = own + c * CS
        bcast(cb[l][:, a:a + CS], cb[l][:, a:a + CS], "%s%d" % ("bc" if l else "ac", c))

    g.wait_ge(sem.dgv, 16)
    bcast(T.gs[:], T.gl[:, 4 * rank:4 * rank + 4], "agv")
    send(0, 0)
    g.wait_ge(sem.von, 1)
    masks(0)
    send(0, 1)
    masks(1)
    send(0, 2)
    masks(2)
    masks(3)
    send(0, 3)
    g.affine_select(T.rm[:], T.ones[:, 0:128], [[-1, 16], [-16, 8]], OP.is_equal, 0.0, 0, 1).then_inc(sem.rmg, 1)
    for c in range(NCH):
        send(1, c)
    g.wait_ge(sem.loc, ne * (1 + 2 * NCH))

    def onehot_wires(l, i):
        k = 2 * l + i
        V.tensor_scalar(T.vt[:, 256 * k:256 * k + 256], T.iotl[:], T.wf[:, k:k + 1], 64.0 if i == 0 else 1.0,
                        OP.is_equal, OP.mult).then_inc(sem["vvt%d" % l], 1)

    def onehot_give(l):
        for k in (2 * l, 2 * l + 1):
            V.tensor_scalar(T.gt[:, 128 * k:128 * k + 128], T.iotn[:], T.giv[:, k:k + 1], None, OP.is_equal).then_inc(sem["vgt%d" % l], 1)

    def fix(c, halves=(0, 1)):
        P.wait_ge(sem["tr%d" % min(c, 2)], 1 if c else 8)
        if c == 0:
            P.wait_ge(sem.vpm, 4)
        if c >= 2:
            P.wait_ge(sem["ce%d" % (c - 2)], 1)
        for h in halves:
            for bp in range(8 if c else 1):
                for g2 in range(2):
                    k = 2 * g2 + h
                    if c:
                        i0 = c * CS + 32 * bp + 16 * g2
                        o, i = psf[c % 2][:, 128 * h + bp:128 * h + 128:8], T.yt[:, i0:i0 + 16]
                    else:
                        o, i = psf[0][:, 128 * h:128 * h + 128], T.yt[:, 128 * g2:128 * g2 + 128]
                    m = P.matmul(o, T.pm[:, 128 * k:128 * k + 128], i, g2 == 0, g2 == 1)
            m.then_inc(sem["pf%d" % c], 1)

    def compose_v(l):
        P.wait_ge(sem["vvt%d" % l], 2)
        for kh in range(2):
            for i in range(2):
                a = (2 * l + i) * 256 + 128 * kh
                m = P.matmul(psv[l][:, 128 * kh:128 * kh + 128], T.vt[:, a:a + 128], T.ident[:], i == 0, i == 1)
                if i == 1:
                    m.then_inc(sem["pv%d" % l], 1)

    def w_part(l, q, kh):
        a = 128 * q if l else 0
        return P.matmul(psw[l][q][:, a:a + 128],
                        T.gt[32 * q:32 * q + 32, (2 * l + kh) * 128:(2 * l + kh) * 128 + 128],
                        T.vb[32 * q:32 * q + 32, l * 256 + 128 * kh:l * 256 + 128 * kh + 128], kh == 0, kh == 1)

    def compose_w0():
        P.wait_ge(sem.sv0, 1)
        for kh in range(2):
            P.wait_ge(sem.vgt0, kh + 1)
            for q in range(4):
                m = w_part(0, q, kh)
                if kh:
                    m.then_inc(sem["pwv" if q < 3 else "pws"], 1)

    def compose_w1():
        P.wait_ge(sem.vgt1, 2)
        P.wait_ge(sem.sv1, 1)
        for q in range(4):
            if q:
                P.wait_ge(sem.pw1, q)
            w_part(1, q, 0)
            w_part(1, q, 1).then_inc(sem.pw1, 1)

    def addresses(l, c):
        P.wait_ge(sem["%s%d" % ("ce" if l == 0 else "sc", c)], 1)
        P.wait_ge(sem["%s%d" % ("ac" if l == 0 else "bc", c)], ne * n_oth)
        if c == 0:
            P.wait_ge(sem.sw1 if l else sem.sv1, 1)
        k = l * NCH + c - 2
        if k >= 0:
            P.wait_ge(sem["ea%d%d" % (k // NCH, k % NCH)], 2)
        for q in range(4):
            if l == 0 and c == 0:
                P.wait_ge(sem.swv if q < 3 else sem.sws, q + 1 if q < 3 else 1)
            m = P.matmul(psa[c % 2][:, 0:CS], T.w[:, (4 * l + q) * 128:(4 * l + q) * 128 + 128],
                         cb[l][:, q * 1024 + c * CS:q * 1024 + (c + 1) * CS], q == 0, q == 3)
        m.then_inc(sem["pa%d%d" % (l, c)], 1)

    def gpos(l, c, h):
        if l == 0 or c < NCH - 1:
            nv = SPL[l][c]
            return (c * CS + nv, (c + 1) * CS) if h else (c * CS, c * CS + nv)
        o = (NCH - 1) * CS + 128 * h
        return (o, o + 8 * SA) if c == NCH - 1 else (o + 8 * SA, o + 128)

    def tile(c, h):
        return gpos(1, c, h) if c >= NCH - 1 else (c * CS + 128 * h, c * CS + 128 * h + 128)

    def pick(l, c):
        if c == 0:
            if l:
                P.wait_ge(sem.rmg, 1)
            else:
                P.wait_ge(sem.lmg, 4)
        k = l * NCH + c - 2
        if k >= 0:
            P.wait_ge(sem["%s%d" % ("sc" if k < NCH else "sy", k % NCH)], 1)
        for h in range(2):
            P.wait_ge(sem["%s%d%d" % ("gs" if h else "gv", l, c)], 1)
            j0, j1 = tile(c, h) if l else gpos(0, c, h)
            if l and h == 0 and j1 > gpos(1, c, 0)[1]:
                P.wait_ge(sem["gs%d%d" % (l, c)], 1)
            for u in range(16):
                src = ga[l][:, 16 * j0 + u:16 * j1:16]
                if l == 0:
                    m = P.matmul(psc[c % 2][:, j0 - c * CS:j1 - c * CS], T.lm[:, 128 * u:128 * u + 128], src, u == 0, u == 15)
                else:
                    m = P.matmul(psc[c % 2][0:j1 - j0, 16 * h + u:256:32], src, T.rm[:, 8 * u:8 * u + 8], True, True)
            m.then_inc(sem["pd%d%d" % (l, c)], 1)

    def evac_addr(l, c):
        V.wait_ge(sem["pa%d%d" % (l, c)], 1)
        for a, b in (gpos(l, c, 0), gpos(l, c, 1)) if SPL[l][c] else ((c * CS, (c + 1) * CS),):
            V.tensor_copy(off[l][:, a:b], psa[c % 2][:, a - c * CS:b - c * CS]).then_inc(sem["ea%d%d" % (l, c)], 1)

    def gather(l, c, h):
        q = S if h else V
        q.wait_ge(sem["ea%d%d" % (l, min(c, NCH - 1))], 2 if h and SPL[l][min(c, NCH - 1)] else 1)
        if c == 0:
            q.wait_ge(sem["dt%d" % l], 16 if l else 32)
        j0, j1 = gpos(l, c, h)
        win = tab[l][:, 0:4096].indirect(off[l][:, j0:j1])
        if h == 0:
            V.tensor_copy(ga[l][:, 16 * j0:16 * j1], win).then_inc(sem["gv%d%d" % (l, c)], 1)
        else:
            S.activation(ga[l][:, 16 * j0:16 * j1], win, ACT.Copy).then_inc(sem["gs%d%d" % (l, c)], 1)

    def s_c0(c):
        S.wait_ge(sem["pf%d" % c], 2)
        S.activation(T.c0[:, own + c * CS:own + (c + 1) * CS], psf[c % 2][:, 0:CS], ACT.Copy).then_inc(sem["ce%d" % c], 1)

    def s_c1(c):
        S.wait_ge(sem["pd0%d" % c], 2)
        S.activation(T.c1[:, own + c * CS:own + (c + 1) * CS], psc[c % 2][:, 0:CS], ACT.Copy).then_inc(sem["sc%d" % c], 1)

    def ysrc(c):
        if c < NCH - 1:
            return T.ys, c * CS, 128
        return (T.ys, (NCH - 1) * CS, 8 * SA) if c == NCH - 1 else (T.yl, 0, 128 - 8 * SA)

    def out_y(q, c):
        q.wait_ge(sem["pd1%d" % c], 2)
        b, a, n = ysrc(c)
        if q is V:
            m = V.tensor_copy(b[0:n, a:a + CS], psc[c % 2][0:n, 0:CS])
        else:
            m = S.activation(b[0:n, a:a + CS], psc[c % 2][0:n, 0:CS], ACT.Copy)
        m.then_inc(sem["sy%d" % c], 1)

    V.memset(T.ones[:], 1.0).then_inc(sem.von, 1)
    V.wait_ge(sem.iop, 1)
    V.tensor_scalar(T.kbi[:], T.pcol[:], 4, 1, OP.logical_shift_right, OP.bitwise_and).then_inc(sem.vi, 1)
    V.wait_ge(sem.vi, 1)
    V.tensor_copy(T.kbf[:, 1:2], T.kbi[:]).then_inc(sem.vf, 1)
    V.tensor_scalar(T.kbf[:, 0:1], T.kbi[:], -1.0, 1.0, OP.mult, OP.add).then_inc(sem.vf, 1)
    V.wait_ge(sem.iod, 1)
    V.tensor_scalar(T.ident[:], T.diff[:], 0.0, None, OP.is_equal).then_inc(sem.vid, 1)
    V.wait_ge(sem.vf, 2)
    for g2 in range(2):
        for h in range(2):
            k = 2 * g2 + h
            V.tensor_scalar(T.pm[:, 128 * k:128 * k + 128], T.diff[:], float(16 * (g2 - h)), T.kbf[:, h:h + 1],
                            OP.is_equal, OP.mult).then_inc(sem.vpm, 1)
    V.wait_ge(sem.dx0, 16)
    for h in range(2):
        V.tensor_copy(T.xb[:, 128 * h:128 * h + 128], T.xi[:, 128 * h:128 * h + 128]).then_inc(sem.cv0, 1)
    V.wait_ge(sem.dwr, 16)
    V.tensor_copy(T.wf[:], T.wi[:]).then_inc(sem.vwf, 1)
    for bp in range(8):
        V.wait_ge(sem.cv0, 1 + bp // 4)
        V.transpose(T.yt[:, bp:CS:8], T.xb[:, 32 * bp:32 * bp + 32]).then_inc(sem.tr0, 1)
    V.wait_ge(sem.iol, 1)
    V.wait_ge(sem.vwf, 1)
    onehot_wires(0, 0)
    V.wait_ge(sem.dxr, 16)
    V.tensor_copy(T.xb[:, CS:2 * CS], T.xi[:, CS:2 * CS]).then_inc(sem.cv1, 1)
    onehot_wires(0, 1)
    V.wait_ge(sem.cv1, 1)
    V.transpose(T.yt[:, CS:2 * CS], T.xb[:, CS:2 * CS]).then_inc(sem.tr1, 1)
    V.tensor_copy(T.xb[:, 2 * CS:1024], T.xi[:, 2 * CS:1024]).then_inc(sem.cv2, 1)
    onehot_wires(1, 0)
    onehot_wires(1, 1)
    V.wait_ge(sem.cv2, 1)
    V.transpose(T.yt[:, 2 * CS:1024], T.xb[:, 2 * CS:1024]).then_inc(sem.tr2, 1)
    V.wait_ge(sem.ion, 1)
    V.wait_ge(sem.dgv, 16)
    V.wait_ge(sem.agv, ne * n_oth)
    for q in range(4):
        r0 = 32 * rank
        src = T.gs[r0:r0 + 32, 0:4] if q == rank else T.gl[r0:r0 + 32, 4 * q:4 * q + 4]
        V.tensor_copy(T.giv[32 * q:32 * q + 32, 0:4], src).then_inc(sem.vgiv, 1)
    V.wait_ge(sem.vgiv, 4)
    onehot_give(0)
    for q in range(3):
        V.wait_ge(sem.pwv, q + 1)
        V.tensor_copy(T.w[:, 128 * q:128 * q + 128], psw[0][q][:, 0:128]).then_inc(sem.swv, 1)
    onehot_give(1)
    for c in range(NCH):
        evac_addr(0, c)
        gather(0, c, 0)
    for c in range(NCH):
        evac_addr(1, c)
        if c == NCH - 1:
            out_y(V, 1)
        gather(1, c, 0)
    out_y(V, 2)
    gather(1, 4, 0)
    out_y(V, 3)
    out_y(V, 4)

    s_c0(0)
    S.wait_ge(sem.pv0, 2)
    S.activation(T.vb[:, 0:256], psv[0][:, 0:256], ACT.Copy).then_inc(sem.sv0, 1)
    s_c0(1)
    S.wait_ge(sem.pv1, 2)
    S.activation(T.vb[:, 256:512], psv[1][:, 0:256], ACT.Copy).then_inc(sem.sv1, 1)
    S.wait_ge(sem.pws, 1)
    S.activation(T.w[:, 384:512], psw[0][3][:, 0:128], ACT.Copy).then_inc(sem.sws, 1)
    s_c0(2)
    gather(0, 0, 1)
    s_c0(3)
    S.wait_ge(sem.pw1, 4)
    S.activation(T.w[:, 512:1024], T.psw[:], ACT.Copy).then_inc(sem.sw1, 1)
    gather(0, 1, 1)
    s_c1(0)
    gather(0, 2, 1)
    s_c1(1)
    gather(0, 3, 1)
    s_c1(2)
    gather(1, 0, 1)
    s_c1(3)
    gather(1, 1, 1)
    out_y(S, 0)
    gather(1, 2, 1)
    gather(1, 3, 1)
    gather(1, 4, 1)

    P.wait_ge(sem.vid, 1)
    fix(0)
    compose_v(0)
    fix(1)
    compose_v(1)
    fix(2, (0,))
    compose_w0()
    fix(2, (1,))
    addresses(0, 0)
    fix(3)
    compose_w1()
    addresses(0, 1)
    pick(0, 0)
    addresses(0, 2)
    pick(0, 1)
    addresses(0, 3)
    pick(0, 2)
    addresses(1, 0)
    pick(0, 3)
    addresses(1, 1)
    pick(1, 0)
    addresses(1, 2)
    pick(1, 1)
    addresses(1, 3)
    pick(1, 2)
    pick(1, 3)
    pick(1, 4)

    Y.wait_ge(sem.ea00, 2)
    Y.dma_start(T.tab1[:], T.tb[:, 65536:131072]).then_inc(sem.dt1, 16)
    for c in range(NCH + 1):
        last = c >= NCH - 1
        Y.wait_ge(sem["sy%d" % c], 1)
        if last:
            S.wait_ge(sem["sy%d" % c], 1)
        b, a, n = ysrc(c)
        cc = min(c, NCH - 1)
        for gg in range(8):
            q = S if last and gg % 2 else Y
            r0 = 16 * gg + (SA if c == NCH else 0)
            q.dma_start(T.y[r0:r0 + n // 8, cc * CS:(cc + 1) * CS], b[0:n, a + 32 * gg:a + 32 * gg + 32]).then_inc(sem.dy, 16)
    Y.wait_ge(sem.dy, 16 * 8 * (NCH + 1))
